import numpy as np
import ml_dtypes


def mxq(x, axis, fmt="e4m3"):
    dtype, down = {"e4m3": (ml_dtypes.float8_e4m3fn, 7), "e5m2": (ml_dtypes.float8_e5m2, 14)}[fmt]
    v = np.moveaxis(np.asarray(x, np.float32).astype(ml_dtypes.bfloat16).astype(np.float64), axis, -1)
    blocks = v.reshape(v.shape[:-1] + (-1, 32))
    amax = np.abs(blocks).max(-1, keepdims=True)
    byte = np.maximum(np.where(amax > 0, np.frexp(amax)[1] - 1 + 127, 0) - down, 1)
    scale = np.exp2(byte - 127.0)
    codes = (blocks / scale).astype(np.float32).astype(dtype).astype(np.float64)
    return np.moveaxis((codes * scale).reshape(v.shape), -1, axis)


WIDE = False


def mx_kscale(k):
    if not WIDE:
        return np.ones(k)
    levels = np.array([10, -10, 5, -5, 0])
    if k % 512:
        return np.exp2(np.random.permutation(np.resize(levels, k // 32))).repeat(32)
    a = np.empty((k // 512, 16))
    for p in range(k // 512):
        a[p, :8] = np.random.permutation(np.resize(levels, 8))
        for g in range(8):
            far = levels[np.abs(levels - a[p, g]) >= 10]
            a[p, g + 8] = far[np.random.randint(len(far))]
    return np.exp2(a.ravel()).repeat(32)


def f64(x):
    return np.asarray(x).astype(np.float64)


def striped(idx):
    return np.tile(np.asarray(idx).reshape(-1, 16).T, (8, 1)).astype(np.uint16)


def unstriped(offs):
    return offs[:16].T.reshape(-1).astype(np.int64)


E2M1 = np.array([0.0, 0.5, 1.0, 1.5, 2.0, 3.0, 4.0, 6.0, -0.0, -0.5, -1.0, -1.5, -2.0, -3.0, -4.0, -6.0])


def pack_weight(w, fmt):
    k, n = w.shape
    w = f64(np.asarray(w, np.float32).astype(ml_dtypes.bfloat16)).reshape(k // 32, 32, n)
    amax = np.abs(w).max(1)
    if fmt == "e4m3":
        byte = np.frexp(amax)[1] - 1 + 127 - 7
    else:
        mant, ex = np.frexp(amax / 6.0)
        byte = np.where(mant > 0.5, ex, ex - 1) + 127
    byte = np.clip(np.where(amax > 0, byte, 1), 1, 254)
    scaled = (w * np.exp2(127.0 - byte)[:, None, :]).reshape(k, n).astype(np.float32)
    by_word = np.ascontiguousarray(scaled.reshape(k // 512, 128, 4, n).transpose(0, 1, 3, 2))
    if fmt == "e4m3":
        words = by_word.astype(ml_dtypes.float8_e4m3fn).view(np.uint8)
    else:
        c = by_word.astype(ml_dtypes.float4_e2m1fn).view(np.uint8) & 0xF
        words = (c[..., 0::2] | (c[..., 1::2] << 4)).reshape(k // 512, 128, 2 * n)
    return np.ascontiguousarray(words), np.ascontiguousarray(byte.astype(np.uint8).reshape(k // 512, 16, n))


def unpack_weight(words, scales, fmt):
    g, _, n = scales.shape
    words = np.ascontiguousarray(words).reshape(g, 128, n, -1)
    if fmt == "e4m3":
        vals = words.view(ml_dtypes.float8_e4m3fn).astype(np.float64)
    else:
        nib = np.empty((g, 128, n, 4), np.uint8)
        nib[..., 0::2] = words & 0xF
        nib[..., 1::2] = words >> 4
        vals = E2M1[nib]
    vals = vals * np.repeat(np.exp2(scales.astype(np.float64) - 127.0), 8, axis=1)[..., None]
    return vals.transpose(0, 1, 3, 2).reshape(g * 512, n)


D, K, T, U, I, E = 512, 512, 2048, 1024, 512, 256


def setup_inputs():
    n = np.random.standard_normal
    idx = np.random.permutation(T)[:I]
    idx2 = np.random.permutation(U)[:I]
    idx3 = np.random.permutation(U)[:I]
    fd = mx_kscale(D)
    fk = mx_kscale(K)
    pagesp = pack_weight(n((D, T)) / fd[:, None], "e2m1")
    wap = pack_weight(n((D, K)) * 1.0 / np.sqrt(D) * fd[:, None], "e4m3")
    notesp = pack_weight(n((D, U)) / fd[:, None], "e4m3")
    wbp = pack_weight(n((D, K)) * 1.0 / np.sqrt(D) * fd[:, None], "e2m1")
    wop = pack_weight(n((K, E)) * 1.0 / np.sqrt(K) / fk[:, None], "e4m3")
    return {
        "pages_words": pagesp[0],
        "pages_scales": pagesp[1],
        "wa_words": wap[0],
        "wa_scales": wap[1],
        "notes_words": notesp[0],
        "notes_scales": notesp[1],
        "wb_words": wbp[0],
        "wb_scales": wbp[1],
        "lam": (np.random.uniform(0.5, 1.5, (K, 1))).astype(np.float32),
        "kf": (np.random.uniform(0.5, 2.0, (K, 1)) * fk[:, None]).astype(np.float32),
        "wo_words": wop[0],
        "wo_scales": wop[1],
        "offs": striped(idx),
        "offs2": striped(idx2),
        "offs3": striped(idx3),
    }


def reference(pages_words, pages_scales, wa_words, wa_scales, notes_words, notes_scales, wb_words, wb_scales, lam, kf, wo_words, wo_scales, offs, offs2, offs3):
    idx = unstriped(offs)
    idx2 = unstriped(offs2)
    idx3 = unstriped(offs3)
    pagesu = unpack_weight(pages_words, pages_scales, "e2m1")
    wau = unpack_weight(wa_words, wa_scales, "e4m3")
    notesu = unpack_weight(notes_words, notes_scales, "e4m3")
    wbu = unpack_weight(wb_words, wb_scales, "e2m1")
    wou = unpack_weight(wo_words, wo_scales, "e4m3")
    pagesidxg = pagesu[:, idx]
    z = wau.T @ pagesidxg
    h1 = wbu.T @ notesu
    r = z - h1[:, idx2]
    f1 = np.zeros((K, U))
    f1[:, idx2] = r
    c1 = h1 + f1 * f64(lam)
    w = c1[:, idx3] * f64(kf)
    wq = mxq(w, 0, "e4m3")
    y = wou.T @ wq
    return y

@@ -1,0 +1,194 @@
+from contextlib import ExitStack
+
+import concourse.mybir as mybir
+
+D, K, T, U, I, E = 512, 512, 2048, 1024, 512, 256
+FLOPS = 2 * D * K * I + 2 * D * K * U + 2 * K * E * I
+
+F32 = mybir.dt.float32
+BF16 = mybir.dt.bfloat16
+I32 = mybir.dt.int32
+U32 = mybir.dt.uint32
+U16 = mybir.dt.uint16
+U8 = mybir.dt.uint8
+FP8X4 = mybir.dt.float8_e4m3fn_x4
+FP4X4 = mybir.dt.float4_e2m1fn_x4
+MULT = mybir.AluOpType.mult
+ADD = mybir.AluOpType.add
+SUB = mybir.AluOpType.subtract
+COPY = mybir.ActivationFunctionType.Copy
+
+P = 128
+PACK = 4
+BANK = 512
+HALF = I // 2
+LIST_COLS = I // 16
+
+
+def tile_attend_pagesreplace_kernel(tc, pages_words, pages_scales, wa_words, wa_scales, notes_words, notes_scales,
+                                     wb_words, wb_scales, lam, kf, wo_words, wo_scales, offs, offs2, offs3, out):
+    nc = tc.nc
+    with ExitStack() as ctx:
+        sb = ctx.enter_context(tc.tile_pool(name="sb", bufs=1))
+        ps = ctx.enter_context(tc.psum_pool(name="ps", bufs=1))
+
+        def tile(name, cols, dtype):
+            return sb.tile([P, cols], dtype, name=name, align_bytes=64)
+
+        def load_words(dst, src):
+            nc.sync.dma_start(out=dst[:].bitcast(I32), in_=src.bitcast(I32))
+
+        def load_scales(dst, src, quads=range(4), queue=nc.sync):
+            for q in quads:
+                queue.dma_start(out=dst[32 * q : 32 * q + 4, :].bitcast(I32), in_=src[0, 4 * q : 4 * q + 4, :].bitcast(I32))
+
+        def deal(dst, src):
+            nc.vector.tensor_copy(out=dst[:].rearrange("p (t m) -> p t m", t=PACK), in_=src[:].rearrange("p (m t) -> p t m", t=PACK))
+
+        list1 = sb.tile([P, LIST_COLS], U16, name="list1")
+        list2 = sb.tile([P, LIST_COLS], U16, name="list2")
+        list3 = sb.tile([P, LIST_COLS], U16, name="list3")
+        pages_w, pages_s = tile("pages_w", T, U16), tile("pages_s", T, U8)
+        notes_w, notes_s = tile("notes_w", U, U32), tile("notes_s", U, U8)
+        wa_w, wa_s = tile("wa_w", K, U32), tile("wa_s", K, U8)
+        wb_w, wb_s = tile("wb_w", K, U16), tile("wb_s", K, U8)
+        wo_w, wo_s = tile("wo_w", E, U32), tile("wo_s", E, U8)
+        lam_t, kf_t = tile("lam_t", PACK, F32), tile("kf_t", PACK, F32)
+
+        for plane in (notes_s, wb_s, wa_s, pages_s, wo_s):
+            nc.vector.memset(plane[:].bitcast(U32), 0)
+
+        load_words(wb_w, wb_words[0])
+        load_words(notes_w, notes_words[0].rearrange("p n t -> p (n t)"))
+        load_scales(wb_s, wb_scales)
+        load_scales(notes_s, notes_scales, range(2))
+        load_scales(notes_s, notes_scales, range(2, 4), nc.gpsimd)
+        load_scales(wa_s, wa_scales, range(4), nc.gpsimd)
+        nc.sync.dma_start(out=list1[:], in_=offs)
+        load_words(pages_w, pages_words[0])
+        load_scales(pages_s, pages_scales)
+        nc.sync.dma_start(out=list2[:], in_=offs2)
+        load_words(wa_w, wa_words[0].rearrange("p n t -> p (n t)"))
+        nc.sync.dma_start(out=lam_t[:], in_=lam.rearrange("(p t) o -> p (t o)", t=PACK))
+        nc.sync.dma_start(out=list3[:], in_=offs3)
+        nc.sync.dma_start(out=kf_t[:], in_=kf.rearrange("(p t) o -> p (t o)", t=PACK))
+        load_words(wo_w, wo_words[0].rearrange("p n t -> p (n t)"))
+        load_scales(wo_s, wo_scales)
+
+        wb_wd, wb_sd = tile("wb_wd", K, U16), tile("wb_sd", K, U8)
+        wa_wd, wa_sd = tile("wa_wd", K, U32), tile("wa_sd", K, U8)
+        picked_w, picked_s = tile("picked_w", I, U16), tile("picked_s", I, U8)
+        h1 = [tile("h1_%d" % t, U, F32) for t in range(PACK)]
+        c1 = [tile("c1_%d" % t, U, F32) for t in range(PACK)]
+        hg = [tile("hg_%d" % t, I, F32) for t in range(PACK)]
+        zr = [tile("zr_%d" % t, I, F32) for t in range(PACK)]
+        cg = [[tile("cg_%d_%d" % (t, a), HALF, F32) for a in range(2)] for t in range(PACK)]
+        woven = [sb.tile([P, HALF, PACK], BF16, name="woven_%d" % a, align_bytes=64) for a in range(2)]
+        wq_w = [tile("wq_w_%d" % a, HALF, U32) for a in range(2)]
+        wq_s = [tile("wq_s_%d" % a, HALF, U8) for a in range(2)]
+        z_bank = {}
+
+        def cols(t):
+            return slice(t * P, (t + 1) * P)
+
+        def hidden_notes(t, engines):
+            for b in range(2):
+                bank = ps.tile([P, BANK], F32, name="h_bank", tag="h%d" % (2 * (t % 2) + b))
+                notes = slice(b * BANK, (b + 1) * BANK)
+                nc.tensor.matmul_mx(out=bank[:], lhsT=wb_wd[:, cols(t)].bitcast(FP4X4), lhsT_scale=wb_sd[:, cols(t)],
+                                    rhs=notes_w[:, notes].bitcast(FP8X4), rhs_scale=notes_s[:, notes], start=True, stop=True)
+                if engines[b] == "S":
+                    nc.scalar.copy(out=h1[t][:, notes], in_=bank[:])
+                else:
+                    nc.vector.tensor_copy(out=h1[t][:, notes], in_=bank[:])
+
+        def hidden_pages(t):
+            z_bank[t] = ps.tile([P, BANK], F32, name="z_bank", tag="z%d" % t)
+            nc.tensor.matmul_mx(out=z_bank[t][:], lhsT=wa_wd[:, cols(t)].bitcast(FP8X4), lhsT_scale=wa_sd[:, cols(t)],
+                                rhs=picked_w[:].bitcast(FP4X4), rhs_scale=picked_s[:], start=True, stop=True)
+
+        def look_up_h1(t, sign):
+            nc.scalar.activation(out=hg[t][:], in_=h1[t][:].indirect(list2[:]), func=COPY, scale=sign)
+
+        def difference(t):
+            nc.vector.tensor_tensor(out=zr[t][:], in0=z_bank[t][:], in1=hg[t][:], op=SUB)
+
+        def scatter_on_scalar(t):
+            for a in range(2):
+                entries = list2[:, a * LIST_COLS // 2 : (a + 1) * LIST_COLS // 2]
+                nc.scalar.activation(out=f1_scalar[:].indirect(entries), in_=zr[t][:, a * HALF : (a + 1) * HALF], func=COPY)
+
+        def copy_z(t):
+            nc.scalar.copy(out=zr[t][:], in_=z_bank[t][:])
+
+        def scatter_on_vector(t):
+            nc.vector.tensor_tensor(out=f1_vector[:].indirect(list2[:]), in0=zr[t][:], in1=hg[t][:], op=ADD)
+
+        def update(t, f1):
+            nc.vector.scalar_tensor_tensor(out=c1[t][:], in0=f1[:], scalar=lam_t[:, t : t + 1], in1=h1[t][:], op0=MULT, op1=ADD)
+
+        def look_up_c1(t):
+            for a in range(2):
+                entries = list3[:, a * LIST_COLS // 2 : (a + 1) * LIST_COLS // 2]
+                nc.scalar.activation(out=cg[t][a][:], in_=c1[t][:].indirect(entries), func=COPY)
+
+        def weave(t, a):
+            nc.vector.tensor_scalar(out=woven[a][:, :, t], in0=cg[t][a][:], scalar1=kf_t[:, t : t + 1], scalar2=None, op0=MULT)
+
+        def finish(a):
+            nc.vector.quantize_mx(out=wq_w[a][:].bitcast(FP8X4), scales=wq_s[a][:], in_=woven[a][:].rearrange("p i t -> p (i t)"))
+            for e in range(2):
+                bank = ps.tile([P, HALF], F32, name="y_bank", tag="h%d" % (2 * a + e))
+                nc.tensor.matmul_mx(out=bank[:], lhsT=wo_w[:, cols(e)].bitcast(FP8X4), lhsT_scale=wo_s[:, cols(e)],
+                                    rhs=wq_w[a][:].bitcast(FP8X4), rhs_scale=wq_s[a][:], start=True, stop=True)
+                y = tile("y_%d_%d" % (a, e), HALF, F32)
+                if a == 1 and e == 1:
+                    nc.vector.tensor_copy(out=y[:], in_=bank[:])
+                else:
+                    nc.scalar.copy(out=y[:], in_=bank[:])
+                nc.sync.dma_start(out=out[cols(e), a * HALF : (a + 1) * HALF], in_=y[:])
+
+        deal(wb_wd, wb_w)
+        deal(wb_sd, wb_s)
+        f1_scalar = sb.tile([P, U], F32, name="f1_scalar", tag="wb_w", align_bytes=64)
+        f1_vector = sb.tile([P, U], F32, name="f1_vector", tag="wb_s", align_bytes=64)
+        nc.vector.memset(f1_scalar[:], 0.0)
+        nc.vector.memset(f1_vector[:], 0.0)
+        hidden_notes(0, "SS")
+        nc.vector.tensor_copy(out=picked_w[:], in_=pages_w[:].indirect(list1[:]))
+        look_up_h1(0, 1.0)
+        nc.vector.tensor_copy(out=picked_s[:], in_=pages_s[:].indirect(list1[:]))
+        hidden_notes(1, "SS")
+        deal(wa_wd, wa_w)
+        deal(wa_sd, wa_s)
+        look_up_h1(1, -1.0)
+        hidden_notes(2, "VV")
+        for t in range(PACK):
+            hidden_pages(t)
+        difference(0)
+        copy_z(1)
+        scatter_on_scalar(0)
+        scatter_on_vector(1)
+        look_up_h1(2, -1.0)
+        copy_z(2)
+        update(0, f1_scalar)
+        update(1, f1_vector)
+        hidden_notes(3, "SS")
+        look_up_h1(3, 1.0)
+        scatter_on_vector(2)
+        look_up_c1(0)
+        look_up_c1(1)
+        difference(3)
+        scatter_on_scalar(3)
+        update(2, f1_vector)
+        for t in range(2):
+            for a in range(2):
+                weave(t, a)
+        look_up_c1(2)
+        update(3, f1_scalar)
+        look_up_c1(3)
+        weave(2, 0)
+        weave(2, 1)
+        for a in range(2):
+            weave(3, a)
+            finish(a)

@@ -23,6 +23,7 @@ PACK = 4
 BANK = 512
 HALF = I // 2
 LIST_COLS = I // 16
+RUN = 4
 
 
 def tile_attend_pagesreplace_kernel(tc, pages_words, pages_scales, wa_words, wa_scales, notes_words, notes_scales,
@@ -38,12 +39,12 @@ def tile_attend_pagesreplace_kernel(tc, pages_words, pages_scales, wa_words, wa_
         def load_words(dst, src):
             nc.sync.dma_start(out=dst[:].bitcast(I32), in_=src.bitcast(I32))
 
-        def load_scales(dst, src, quads=range(4), queue=nc.sync):
+        def load_scales(dst, src, quads=range(4)):
             for q in quads:
-                queue.dma_start(out=dst[32 * q : 32 * q + 4, :].bitcast(I32), in_=src[0, 4 * q : 4 * q + 4, :].bitcast(I32))
+                nc.sync.dma_start(out=dst[32 * q : 32 * q + 32, :].bitcast(I32), in_=src[0, 4 * q : 4 * q + 4, :].bitcast(I32).partition_broadcast(8))
 
         def deal(dst, src):
-            nc.vector.tensor_copy(out=dst[:].rearrange("p (t m) -> p t m", t=PACK), in_=src[:].rearrange("p (m t) -> p t m", t=PACK))
+            nc.vector.tensor_copy(out=dst[:].rearrange("p (t m) -> p m t", t=PACK), in_=src[:].rearrange("p (m t) -> p m t", t=PACK))
 
         list1 = sb.tile([P, LIST_COLS], U16, name="list1")
         list2 = sb.tile([P, LIST_COLS], U16, name="list2")
@@ -54,21 +55,23 @@ def tile_attend_pagesreplace_kernel(tc, pages_words, pages_scales, wa_words, wa_
         wb_w, wb_s = tile("wb_w", K, U16), tile("wb_s", K, U8)
         wo_w, wo_s = tile("wo_w", E, U32), tile("wo_s", E, U8)
         lam_t, kf_t = tile("lam_t", PACK, F32), tile("kf_t", PACK, F32)
+        windows = [tile("f1_%d" % n, U, F32) for n in range(3)]
+        f1 = [windows[t % 3] for t in range(PACK)]
 
-        for plane in (notes_s, wb_s, wa_s, pages_s, wo_s):
-            nc.vector.memset(plane[:].bitcast(U32), 0)
+        for window in windows:
+            nc.vector.memset(window[:], 0.0)
 
-        load_words(wb_w, wb_words[0])
-        load_words(notes_w, notes_words[0].rearrange("p n t -> p (n t)"))
         load_scales(wb_s, wb_scales)
+        load_words(wb_w, wb_words[0])
         load_scales(notes_s, notes_scales, range(2))
-        load_scales(notes_s, notes_scales, range(2, 4), nc.gpsimd)
-        load_scales(wa_s, wa_scales, range(4), nc.gpsimd)
+        load_words(notes_w, notes_words[0].rearrange("p n t -> p (n t)"))
+        load_scales(notes_s, notes_scales, range(2, 4))
         nc.sync.dma_start(out=list1[:], in_=offs)
         load_words(pages_w, pages_words[0])
-        load_scales(pages_s, pages_scales)
+        load_scales(wa_s, wa_scales)
         nc.sync.dma_start(out=list2[:], in_=offs2)
         load_words(wa_w, wa_words[0].rearrange("p n t -> p (n t)"))
+        load_scales(pages_s, pages_scales)
         nc.sync.dma_start(out=lam_t[:], in_=lam.rearrange("(p t) o -> p (t o)", t=PACK))
         nc.sync.dma_start(out=list3[:], in_=offs3)
         nc.sync.dma_start(out=kf_t[:], in_=kf.rearrange("(p t) o -> p (t o)", t=PACK))
@@ -80,115 +83,114 @@ def tile_attend_pagesreplace_kernel(tc, pages_words, pages_scales, wa_words, wa_
         picked_w, picked_s = tile("picked_w", I, U16), tile("picked_s", I, U8)
         h1 = [tile("h1_%d" % t, U, F32) for t in range(PACK)]
         c1 = [tile("c1_%d" % t, U, F32) for t in range(PACK)]
-        hg = [tile("hg_%d" % t, I, F32) for t in range(PACK)]
-        zr = [tile("zr_%d" % t, I, F32) for t in range(PACK)]
-        cg = [[tile("cg_%d_%d" % (t, a), HALF, F32) for a in range(2)] for t in range(PACK)]
-        woven = [sb.tile([P, HALF, PACK], BF16, name="woven_%d" % a, align_bytes=64) for a in range(2)]
+        r = [tile("r_%d" % t, I, F32) for t in range(PACK)]
+        cg = [sb.tile([P, PACK, HALF], F32, name="cg_%d" % a, align_bytes=64) for a in range(2)]
+        woven = [tile("woven_%d" % a, HALF * PACK, BF16) for a in range(2)]
         wq_w = [tile("wq_w_%d" % a, HALF, U32) for a in range(2)]
         wq_s = [tile("wq_s_%d" % a, HALF, U8) for a in range(2)]
-        z_bank = {}
+        z_bank, hg = {}, {}
 
         def cols(t):
             return slice(t * P, (t + 1) * P)
 
-        def hidden_notes(t, engines):
+        def slots(a):
+            return slice(a * HALF, (a + 1) * HALF)
+
+        def entries(offsets, a):
+            return offsets[:, a * LIST_COLS // 2 : (a + 1) * LIST_COLS // 2]
+
+        def bank_tile(n, width=BANK):
+            return ps.tile([P, width], F32, name="bank", tag="bank%d" % n)
+
+        def move(engine, dst, src):
+            if engine == "S":
+                nc.scalar.activation(out=dst, in_=src, func=COPY)
+            else:
+                nc.vector.tensor_copy(out=dst, in_=src)
+
+        def hidden_notes(t, banks, engine):
             for b in range(2):
-                bank = ps.tile([P, BANK], F32, name="h_bank", tag="h%d" % (2 * (t % 2) + b))
+                bank = bank_tile(banks[b])
                 notes = slice(b * BANK, (b + 1) * BANK)
                 nc.tensor.matmul_mx(out=bank[:], lhsT=wb_wd[:, cols(t)].bitcast(FP4X4), lhsT_scale=wb_sd[:, cols(t)],
                                     rhs=notes_w[:, notes].bitcast(FP8X4), rhs_scale=notes_s[:, notes], start=True, stop=True)
-                if engines[b] == "S":
-                    nc.scalar.copy(out=h1[t][:, notes], in_=bank[:])
-                else:
-                    nc.vector.tensor_copy(out=h1[t][:, notes], in_=bank[:])
+                move(engine, h1[t][:, notes], bank[:])
 
         def hidden_pages(t):
-            z_bank[t] = ps.tile([P, BANK], F32, name="z_bank", tag="z%d" % t)
+            z_bank[t] = bank_tile(4 + t)
             nc.tensor.matmul_mx(out=z_bank[t][:], lhsT=wa_wd[:, cols(t)].bitcast(FP8X4), lhsT_scale=wa_sd[:, cols(t)],
                                 rhs=picked_w[:].bitcast(FP4X4), rhs_scale=picked_s[:], start=True, stop=True)
 
-        def look_up_h1(t, sign):
-            nc.scalar.activation(out=hg[t][:], in_=h1[t][:].indirect(list2[:]), func=COPY, scale=sign)
+        def look_up_h1(t, engine, buffer):
+            hg[t] = sb.tile([P, I], F32, name="hg", tag="hg%d" % buffer, align_bytes=64)
+            move(engine, hg[t][:], h1[t][:].indirect(list2[:]))
 
         def difference(t):
-            nc.vector.tensor_tensor(out=zr[t][:], in0=z_bank[t][:], in1=hg[t][:], op=SUB)
+            nc.vector.tensor_tensor(out=r[t][:], in0=z_bank[t][:], in1=hg[t][:], op=SUB)
 
-        def scatter_on_scalar(t):
-            for a in range(2):
-                entries = list2[:, a * LIST_COLS // 2 : (a + 1) * LIST_COLS // 2]
-                nc.scalar.activation(out=f1_scalar[:].indirect(entries), in_=zr[t][:, a * HALF : (a + 1) * HALF], func=COPY)
+        def scatter(t, engine):
+            if engine == "S":
+                for a in range(2):
+                    move("S", f1[t][:].indirect(entries(list2, a)), r[t][:, slots(a)])
+            else:
+                move("V", f1[t][:].indirect(list2[:]), r[t][:])
 
-        def copy_z(t):
-            nc.scalar.copy(out=zr[t][:], in_=z_bank[t][:])
+        def update(t):
+            nc.vector.scalar_tensor_tensor(out=c1[t][:], in0=f1[t][:], scalar=lam_t[:, t : t + 1], in1=h1[t][:], op0=MULT, op1=ADD)
 
-        def scatter_on_vector(t):
-            nc.vector.tensor_tensor(out=f1_vector[:].indirect(list2[:]), in0=zr[t][:], in1=hg[t][:], op=ADD)
+        def look_up_c1(t, a, engine):
+            move(engine, cg[a][:, t, :], c1[t][:].indirect(entries(list3, a)))
 
-        def update(t, f1):
-            nc.vector.scalar_tensor_tensor(out=c1[t][:], in0=f1[:], scalar=lam_t[:, t : t + 1], in1=h1[t][:], op0=MULT, op1=ADD)
-
-        def look_up_c1(t):
-            for a in range(2):
-                entries = list3[:, a * LIST_COLS // 2 : (a + 1) * LIST_COLS // 2]
-                nc.scalar.activation(out=cg[t][a][:], in_=c1[t][:].indirect(entries), func=COPY)
-
-        def weave(t, a):
-            nc.vector.tensor_scalar(out=woven[a][:, :, t], in0=cg[t][a][:], scalar1=kf_t[:, t : t + 1], scalar2=None, op0=MULT)
+        def weave(a):
+            nc.vector.tensor_tensor(out=woven[a][:].rearrange("p (c i t) -> p c t i", i=RUN, t=PACK),
+                                    in0=cg[a][:].rearrange("p t (c i) -> p c t i", i=RUN),
+                                    in1=kf_t[:].unsqueeze(1).unsqueeze(3).to_broadcast([P, HALF // RUN, PACK, RUN]), op=MULT)
 
         def finish(a):
-            nc.vector.quantize_mx(out=wq_w[a][:].bitcast(FP8X4), scales=wq_s[a][:], in_=woven[a][:].rearrange("p i t -> p (i t)"))
+            nc.vector.quantize_mx(out=wq_w[a][:].bitcast(FP8X4), scales=wq_s[a][:], in_=woven[a][:])
             for e in range(2):
-                bank = ps.tile([P, HALF], F32, name="y_bank", tag="h%d" % (2 * a + e))
+                bank = bank_tile(2 * a + e, HALF)
                 nc.tensor.matmul_mx(out=bank[:], lhsT=wo_w[:, cols(e)].bitcast(FP8X4), lhsT_scale=wo_s[:, cols(e)],
                                     rhs=wq_w[a][:].bitcast(FP8X4), rhs_scale=wq_s[a][:], start=True, stop=True)
                 y = tile("y_%d_%d" % (a, e), HALF, F32)
-                if a == 1 and e == 1:
-                    nc.vector.tensor_copy(out=y[:], in_=bank[:])
-                else:
-                    nc.scalar.copy(out=y[:], in_=bank[:])
-                nc.sync.dma_start(out=out[cols(e), a * HALF : (a + 1) * HALF], in_=y[:])
+                move("V" if a == 1 and e == 1 else "S", y[:], bank[:])
+                nc.sync.dma_start(out=out[cols(e), slots(a)], in_=y[:])
 
         deal(wb_wd, wb_w)
         deal(wb_sd, wb_s)
-        f1_scalar = sb.tile([P, U], F32, name="f1_scalar", tag="wb_w", align_bytes=64)
-        f1_vector = sb.tile([P, U], F32, name="f1_vector", tag="wb_s", align_bytes=64)
-        nc.vector.memset(f1_scalar[:], 0.0)
-        nc.vector.memset(f1_vector[:], 0.0)
-        hidden_notes(0, "SS")
+        hidden_notes(0, (0, 1), "S")
         nc.vector.tensor_copy(out=picked_w[:], in_=pages_w[:].indirect(list1[:]))
-        look_up_h1(0, 1.0)
-        nc.vector.tensor_copy(out=picked_s[:], in_=pages_s[:].indirect(list1[:]))
-        hidden_notes(1, "SS")
-        deal(wa_wd, wa_w)
+        look_up_h1(0, "S", 0)
         deal(wa_sd, wa_s)
-        look_up_h1(1, -1.0)
-        hidden_notes(2, "VV")
-        for t in range(PACK):
+        deal(wa_wd, wa_w)
+        nc.vector.tensor_copy(out=picked_s[:], in_=pages_s[:].indirect(list1[:]))
+        hidden_notes(1, (2, 3), "S")
+        hidden_notes(2, (0, 1), "V")
+        look_up_h1(1, "S", 1)
+        hidden_notes(3, (2, 3), "V")
+        for t in (0, 2, 1, 3):
             hidden_pages(t)
+        look_up_h1(2, "S", 2)
+        look_up_h1(3, "S", 3)
         difference(0)
-        copy_z(1)
-        scatter_on_scalar(0)
-        scatter_on_vector(1)
-        look_up_h1(2, -1.0)
-        copy_z(2)
-        update(0, f1_scalar)
-        update(1, f1_vector)
-        hidden_notes(3, "SS")
-        look_up_h1(3, 1.0)
-        scatter_on_vector(2)
-        look_up_c1(0)
-        look_up_c1(1)
+        scatter(0, "S")
+        difference(2)
+        difference(1)
         difference(3)
-        scatter_on_scalar(3)
-        update(2, f1_vector)
-        for t in range(2):
-            for a in range(2):
-                weave(t, a)
-        look_up_c1(2)
-        update(3, f1_scalar)
-        look_up_c1(3)
-        weave(2, 0)
-        weave(2, 1)
+        scatter(1, "V")
+        scatter(2, "S")
+        update(0)
+        scatter(3, "S")
+        update(1)
+        look_up_c1(0, 0, "V")
+        look_up_c1(0, 1, "V")
+        update(2)
+        update(3)
         for a in range(2):
-            weave(3, a)
+            look_up_c1(1, a, "S")
+            look_up_c1(2, a, "S")
+        look_up_c1(3, 0, "V")
+        look_up_c1(3, 1, "S")
+        for a in range(2):
+            weave(a)
             finish(a)

@@ -23,7 +23,7 @@ PACK = 4
 BANK = 512
 HALF = I // 2
 LIST_COLS = I // 16
-RUN = 4
+RUN = 2
 
 
 def tile_attend_pagesreplace_kernel(tc, pages_words, pages_scales, wa_words, wa_scales, notes_words, notes_scales,
@@ -41,10 +41,11 @@ def tile_attend_pagesreplace_kernel(tc, pages_words, pages_scales, wa_words, wa_
 
         def load_scales(dst, src, quads=range(4)):
             for q in quads:
-                nc.sync.dma_start(out=dst[32 * q : 32 * q + 32, :].bitcast(I32), in_=src[0, 4 * q : 4 * q + 4, :].bitcast(I32).partition_broadcast(8))
+                nc.sync.dma_start(out=dst[32 * q : 32 * q + 4, :].bitcast(I32), in_=src[0, 4 * q : 4 * q + 4, :].bitcast(I32))
 
-        def deal(dst, src):
-            nc.vector.tensor_copy(out=dst[:].rearrange("p (t m) -> p m t", t=PACK), in_=src[:].rearrange("p (m t) -> p m t", t=PACK))
+        def deal(dst, src, run):
+            nc.vector.tensor_copy(out=dst[:].rearrange("p (t c i) -> p c t i", t=PACK, i=run),
+                                  in_=src[:].rearrange("p (c i t) -> p c t i", t=PACK, i=run))
 
         list1 = sb.tile([P, LIST_COLS], U16, name="list1")
         list2 = sb.tile([P, LIST_COLS], U16, name="list2")
@@ -55,23 +56,23 @@ def tile_attend_pagesreplace_kernel(tc, pages_words, pages_scales, wa_words, wa_
         wb_w, wb_s = tile("wb_w", K, U16), tile("wb_s", K, U8)
         wo_w, wo_s = tile("wo_w", E, U32), tile("wo_s", E, U8)
         lam_t, kf_t = tile("lam_t", PACK, F32), tile("kf_t", PACK, F32)
-        windows = [tile("f1_%d" % n, U, F32) for n in range(3)]
-        f1 = [windows[t % 3] for t in range(PACK)]
+        f1 = {0: tile("f1_0", U, F32)}
 
-        for window in windows:
-            nc.vector.memset(window[:], 0.0)
+        for plane in (wb_s, pages_s, wa_s):
+            nc.vector.memset(plane[:].bitcast(U32), 0)
+        nc.vector.memset(f1[0][:], 0.0)
 
-        load_scales(wb_s, wb_scales)
         load_words(wb_w, wb_words[0])
         load_scales(notes_s, notes_scales, range(2))
+        load_scales(wb_s, wb_scales)
         load_words(notes_w, notes_words[0].rearrange("p n t -> p (n t)"))
         load_scales(notes_s, notes_scales, range(2, 4))
         nc.sync.dma_start(out=list1[:], in_=offs)
         load_words(pages_w, pages_words[0])
-        load_scales(wa_s, wa_scales)
         nc.sync.dma_start(out=list2[:], in_=offs2)
-        load_words(wa_w, wa_words[0].rearrange("p n t -> p (n t)"))
         load_scales(pages_s, pages_scales)
+        load_words(wa_w, wa_words[0].rearrange("p n t -> p (n t)"))
+        load_scales(wa_s, wa_scales)
         nc.sync.dma_start(out=lam_t[:], in_=lam.rearrange("(p t) o -> p (t o)", t=PACK))
         nc.sync.dma_start(out=list3[:], in_=offs3)
         nc.sync.dma_start(out=kf_t[:], in_=kf.rearrange("(p t) o -> p (t o)", t=PACK))
@@ -81,8 +82,7 @@ def tile_attend_pagesreplace_kernel(tc, pages_words, pages_scales, wa_words, wa_
         wb_wd, wb_sd = tile("wb_wd", K, U16), tile("wb_sd", K, U8)
         wa_wd, wa_sd = tile("wa_wd", K, U32), tile("wa_sd", K, U8)
         picked_w, picked_s = tile("picked_w", I, U16), tile("picked_s", I, U8)
-        h1 = [tile("h1_%d" % t, U, F32) for t in range(PACK)]
-        c1 = [tile("c1_%d" % t, U, F32) for t in range(PACK)]
+        h1, c1 = {}, {}
         r = [tile("r_%d" % t, I, F32) for t in range(PACK)]
         cg = [sb.tile([P, PACK, HALF], F32, name="cg_%d" % a, align_bytes=64) for a in range(2)]
         woven = [tile("woven_%d" % a, HALF * PACK, BF16) for a in range(2)]
@@ -108,34 +108,35 @@ def tile_attend_pagesreplace_kernel(tc, pages_words, pages_scales, wa_words, wa_
             else:
                 nc.vector.tensor_copy(out=dst, in_=src)
 
-        def hidden_notes(t, banks, engine):
+        def hidden_notes(t, banks, engines, buffer):
+            h1[t] = tile(buffer, U, F32)
             for b in range(2):
                 bank = bank_tile(banks[b])
                 notes = slice(b * BANK, (b + 1) * BANK)
                 nc.tensor.matmul_mx(out=bank[:], lhsT=wb_wd[:, cols(t)].bitcast(FP4X4), lhsT_scale=wb_sd[:, cols(t)],
                                     rhs=notes_w[:, notes].bitcast(FP8X4), rhs_scale=notes_s[:, notes], start=True, stop=True)
-                move(engine, h1[t][:, notes], bank[:])
+                move(engines[b], h1[t][:, notes], bank[:])
 
         def hidden_pages(t):
             z_bank[t] = bank_tile(4 + t)
             nc.tensor.matmul_mx(out=z_bank[t][:], lhsT=wa_wd[:, cols(t)].bitcast(FP8X4), lhsT_scale=wa_sd[:, cols(t)],
                                 rhs=picked_w[:].bitcast(FP4X4), rhs_scale=picked_s[:], start=True, stop=True)
 
-        def look_up_h1(t, engine, buffer):
-            hg[t] = sb.tile([P, I], F32, name="hg", tag="hg%d" % buffer, align_bytes=64)
-            move(engine, hg[t][:], h1[t][:].indirect(list2[:]))
+        def look_up_h1(t, sign, buffer):
+            hg[t] = tile(buffer, I, F32)
+            nc.scalar.activation(out=hg[t][:], in_=h1[t][:].indirect(list2[:]), func=COPY, scale=sign)
+
+        def copy_z(t):
+            move("S", r[t][:], z_bank[t][:])
 
         def difference(t):
             nc.vector.tensor_tensor(out=r[t][:], in0=z_bank[t][:], in1=hg[t][:], op=SUB)
 
-        def scatter(t, engine):
-            if engine == "S":
-                for a in range(2):
-                    move("S", f1[t][:].indirect(entries(list2, a)), r[t][:, slots(a)])
-            else:
-                move("V", f1[t][:].indirect(list2[:]), r[t][:])
+        def scatter_half(t, a):
+            move("S", f1[t][:].indirect(entries(list2, a)), r[t][:, slots(a)])
 
-        def update(t):
+        def update(t, buffer):
+            c1[t] = tile(buffer, U, F32)
             nc.vector.scalar_tensor_tensor(out=c1[t][:], in0=f1[t][:], scalar=lam_t[:, t : t + 1], in1=h1[t][:], op0=MULT, op1=ADD)
 
         def look_up_c1(t, a, engine):
@@ -153,44 +154,50 @@ def tile_attend_pagesreplace_kernel(tc, pages_words, pages_scales, wa_words, wa_
                 nc.tensor.matmul_mx(out=bank[:], lhsT=wo_w[:, cols(e)].bitcast(FP8X4), lhsT_scale=wo_s[:, cols(e)],
                                     rhs=wq_w[a][:].bitcast(FP8X4), rhs_scale=wq_s[a][:], start=True, stop=True)
                 y = tile("y_%d_%d" % (a, e), HALF, F32)
-                move("V" if a == 1 and e == 1 else "S", y[:], bank[:])
+                move("SV"[e], y[:], bank[:])
                 nc.sync.dma_start(out=out[cols(e), slots(a)], in_=y[:])
 
-        deal(wb_wd, wb_w)
-        deal(wb_sd, wb_s)
-        hidden_notes(0, (0, 1), "S")
+        deal(wb_wd, wb_w, 8)
+        deal(wb_sd, wb_s, 16)
+        f1[1] = f1[3] = sb.tile([P, U], F32, name="f1_1", tag="wb_w", align_bytes=64)
+        f1[2] = sb.tile([P, U], F32, name="f1_2", tag="wb_s", align_bytes=64)
+        nc.vector.memset(f1[1][:], 0.0)
+        nc.vector.memset(f1[2][:], 0.0)
+        hidden_notes(0, (0, 1), "SS", "h1_0")
         nc.vector.tensor_copy(out=picked_w[:], in_=pages_w[:].indirect(list1[:]))
-        look_up_h1(0, "S", 0)
-        deal(wa_sd, wa_s)
-        deal(wa_wd, wa_w)
+        look_up_h1(0, 1.0, "hg_0")
         nc.vector.tensor_copy(out=picked_s[:], in_=pages_s[:].indirect(list1[:]))
-        hidden_notes(1, (2, 3), "S")
-        hidden_notes(2, (0, 1), "V")
-        look_up_h1(1, "S", 1)
-        hidden_notes(3, (2, 3), "V")
-        for t in (0, 2, 1, 3):
+        deal(wa_wd, wa_w, 4)
+        deal(wa_sd, wa_s, 16)
+        hidden_notes(1, (2, 3), "SS", "h1_1")
+        hidden_notes(2, (0, 1), "VV", "wa_s")
+        look_up_h1(1, 1.0, "hg_1")
+        hidden_notes(3, (2, 3), "SS", "h1_3")
+        for t in range(PACK):
             hidden_pages(t)
-        look_up_h1(2, "S", 2)
-        look_up_h1(3, "S", 3)
+        look_up_h1(2, 1.0, "hg_2")
+        look_up_h1(3, -1.0, "hg_3")
         difference(0)
-        scatter(0, "S")
-        difference(2)
         difference(1)
-        difference(3)
-        scatter(1, "V")
-        scatter(2, "S")
-        update(0)
-        scatter(3, "S")
-        update(1)
-        look_up_c1(0, 0, "V")
-        look_up_c1(0, 1, "V")
-        update(2)
-        update(3)
+        scatter_half(0, 0)
+        difference(2)
+        move("V", f1[1][:].indirect(list2[:]), r[1][:])
+        copy_z(3)
+        scatter_half(0, 1)
+        scatter_half(2, 0)
+        update(1, "c1_1")
+        look_up_c1(1, 0, "S")
+        scatter_half(2, 1)
+        nc.vector.tensor_tensor(out=f1[3][:].indirect(list2[:]), in0=r[3][:], in1=hg[3][:], op=ADD)
+        update(0, "hg_3")
+        look_up_c1(1, 1, "S")
+        update(3, "c1_3")
         for a in range(2):
-            look_up_c1(1, a, "S")
-            look_up_c1(2, a, "S")
-        look_up_c1(3, 0, "V")
-        look_up_c1(3, 1, "S")
+            look_up_c1(0, a, "S")
+        update(2, "r_3")
+        for t in (3, 2):
+            look_up_c1(t, 0, "V")
+            look_up_c1(t, 1, "S")
         for a in range(2):
             weave(a)
             finish(a)

@@ -20,10 +20,12 @@ COPY = mybir.ActivationFunctionType.Copy
 
 P = 128
 PACK = 4
+QUADRANTS = 4
 BANK = 512
 HALF = I // 2
 LIST_COLS = I // 16
-RUN = 2
+LINE = 16
+FIRST_Z_BANK = 4
 
 
 def tile_attend_pagesreplace_kernel(tc, pages_words, pages_scales, wa_words, wa_scales, notes_words, notes_scales,
@@ -33,19 +35,33 @@ def tile_attend_pagesreplace_kernel(tc, pages_words, pages_scales, wa_words, wa_
         sb = ctx.enter_context(tc.tile_pool(name="sb", bufs=1))
         ps = ctx.enter_context(tc.psum_pool(name="ps", bufs=1))
 
-        def tile(name, cols, dtype):
-            return sb.tile([P, cols], dtype, name=name, align_bytes=64)
+        def tile(name, width, dtype, after=None):
+            return sb.tile([P, width], dtype, name=name, tag=after or name, align_bytes=64)
+
+        def bank_tile(n, width):
+            return ps.tile([P, width], F32, name="bank", tag="bank%d" % n)
+
+        def cols(n):
+            return slice(n * P, (n + 1) * P)
+
+        def slots(half):
+            return slice(half * HALF, (half + 1) * HALF)
+
+        def entries(offsets, half):
+            return offsets[:, half * LIST_COLS // 2 : (half + 1) * LIST_COLS // 2]
+
+        def move(engine, dst, src):
+            if engine == "S":
+                nc.scalar.activation(out=dst, in_=src, func=COPY)
+            else:
+                nc.vector.tensor_copy(out=dst, in_=src)
 
         def load_words(dst, src):
             nc.sync.dma_start(out=dst[:].bitcast(I32), in_=src.bitcast(I32))
 
-        def load_scales(dst, src, quads=range(4)):
-            for q in quads:
+        def load_scales(dst, src, quadrants=range(QUADRANTS)):
+            for q in quadrants:
                 nc.sync.dma_start(out=dst[32 * q : 32 * q + 4, :].bitcast(I32), in_=src[0, 4 * q : 4 * q + 4, :].bitcast(I32))
-
-        def deal(dst, src, run):
-            nc.vector.tensor_copy(out=dst[:].rearrange("p (t c i) -> p c t i", t=PACK, i=run),
-                                  in_=src[:].rearrange("p (c i t) -> p c t i", t=PACK, i=run))
 
         list1 = sb.tile([P, LIST_COLS], U16, name="list1")
         list2 = sb.tile([P, LIST_COLS], U16, name="list2")
@@ -63,10 +79,10 @@ def tile_attend_pagesreplace_kernel(tc, pages_words, pages_scales, wa_words, wa_
         nc.vector.memset(f1[0][:], 0.0)
 
         load_words(wb_w, wb_words[0])
-        load_scales(notes_s, notes_scales, range(2))
+        load_scales(notes_s, notes_scales, range(QUADRANTS // 2))
         load_scales(wb_s, wb_scales)
         load_words(notes_w, notes_words[0].rearrange("p n t -> p (n t)"))
-        load_scales(notes_s, notes_scales, range(2, 4))
+        load_scales(notes_s, notes_scales, range(QUADRANTS // 2, QUADRANTS))
         nc.sync.dma_start(out=list1[:], in_=offs)
         load_words(pages_w, pages_words[0])
         nc.sync.dma_start(out=list2[:], in_=offs2)
@@ -79,125 +95,113 @@ def tile_attend_pagesreplace_kernel(tc, pages_words, pages_scales, wa_words, wa_
         load_words(wo_w, wo_words[0].rearrange("p n t -> p (n t)"))
         load_scales(wo_s, wo_scales)
 
-        wb_wd, wb_sd = tile("wb_wd", K, U16), tile("wb_sd", K, U8)
-        wa_wd, wa_sd = tile("wa_wd", K, U32), tile("wa_sd", K, U8)
+        wb_w_dealt, wb_s_dealt = tile("wb_w_dealt", K, U16), tile("wb_s_dealt", K, U8)
+        wa_w_dealt, wa_s_dealt = tile("wa_w_dealt", K, U32), tile("wa_s_dealt", K, U8)
         picked_w, picked_s = tile("picked_w", I, U16), tile("picked_s", I, U8)
-        h1, c1 = {}, {}
-        r = [tile("r_%d" % t, I, F32) for t in range(PACK)]
-        cg = [sb.tile([P, PACK, HALF], F32, name="cg_%d" % a, align_bytes=64) for a in range(2)]
-        woven = [tile("woven_%d" % a, HALF * PACK, BF16) for a in range(2)]
-        wq_w = [tile("wq_w_%d" % a, HALF, U32) for a in range(2)]
-        wq_s = [tile("wq_s_%d" % a, HALF, U8) for a in range(2)]
-        z_bank, hg = {}, {}
+        r = [tile("r_%d" % t, I, F32) for t in range(PACK - 1)]
+        z_last = tile("z_last", I, F32)
+        c1_picked = [sb.tile([P, PACK, HALF], F32, name="c1_picked_%d" % half, align_bytes=64) for half in range(2)]
+        w = [tile("w_%d" % half, HALF * PACK, BF16) for half in range(2)]
+        wq_w = [tile("wq_w_%d" % half, HALF, U32) for half in range(2)]
+        wq_s = [tile("wq_s_%d" % half, HALF, U8) for half in range(2)]
+        h1, c1, z_bank, h1_picked = {}, {}, {}, {}
 
-        def cols(t):
-            return slice(t * P, (t + 1) * P)
+        def deal(dst, src, item_bytes):
+            run = LINE // item_bytes
+            nc.vector.tensor_copy(out=dst[:].rearrange("p (t c i) -> p c t i", t=PACK, i=run),
+                                  in_=src[:].rearrange("p (c i t) -> p c t i", t=PACK, i=run))
 
-        def slots(a):
-            return slice(a * HALF, (a + 1) * HALF)
-
-        def entries(offsets, a):
-            return offsets[:, a * LIST_COLS // 2 : (a + 1) * LIST_COLS // 2]
-
-        def bank_tile(n, width=BANK):
-            return ps.tile([P, width], F32, name="bank", tag="bank%d" % n)
-
-        def move(engine, dst, src):
-            if engine == "S":
-                nc.scalar.activation(out=dst, in_=src, func=COPY)
-            else:
-                nc.vector.tensor_copy(out=dst, in_=src)
-
-        def hidden_notes(t, banks, engines, buffer):
-            h1[t] = tile(buffer, U, F32)
-            for b in range(2):
-                bank = bank_tile(banks[b])
+        def hidden_notes(t, engine, after=None):
+            h1[t] = tile("h1_%d" % t, U, F32, after)
+            for b in range(U // BANK):
+                bank = bank_tile(2 * (t % 2) + b, BANK)
                 notes = slice(b * BANK, (b + 1) * BANK)
-                nc.tensor.matmul_mx(out=bank[:], lhsT=wb_wd[:, cols(t)].bitcast(FP4X4), lhsT_scale=wb_sd[:, cols(t)],
+                nc.tensor.matmul_mx(out=bank[:], lhsT=wb_w_dealt[:, cols(t)].bitcast(FP4X4), lhsT_scale=wb_s_dealt[:, cols(t)],
                                     rhs=notes_w[:, notes].bitcast(FP8X4), rhs_scale=notes_s[:, notes], start=True, stop=True)
-                move(engines[b], h1[t][:, notes], bank[:])
+                move(engine, h1[t][:, notes], bank[:])
 
         def hidden_pages(t):
-            z_bank[t] = bank_tile(4 + t)
-            nc.tensor.matmul_mx(out=z_bank[t][:], lhsT=wa_wd[:, cols(t)].bitcast(FP8X4), lhsT_scale=wa_sd[:, cols(t)],
+            z_bank[t] = bank_tile(FIRST_Z_BANK + t, I)
+            nc.tensor.matmul_mx(out=z_bank[t][:], lhsT=wa_w_dealt[:, cols(t)].bitcast(FP8X4), lhsT_scale=wa_s_dealt[:, cols(t)],
                                 rhs=picked_w[:].bitcast(FP4X4), rhs_scale=picked_s[:], start=True, stop=True)
 
-        def look_up_h1(t, sign, buffer):
-            hg[t] = tile(buffer, I, F32)
-            nc.scalar.activation(out=hg[t][:], in_=h1[t][:].indirect(list2[:]), func=COPY, scale=sign)
-
-        def copy_z(t):
-            move("S", r[t][:], z_bank[t][:])
+        def look_up_h1(t, sign):
+            h1_picked[t] = tile("h1_picked_%d" % t, I, F32)
+            nc.scalar.activation(out=h1_picked[t][:], in_=h1[t][:].indirect(list2[:]), func=COPY, scale=sign)
 
         def difference(t):
-            nc.vector.tensor_tensor(out=r[t][:], in0=z_bank[t][:], in1=hg[t][:], op=SUB)
+            nc.vector.tensor_tensor(out=r[t][:], in0=z_bank[t][:], in1=h1_picked[t][:], op=SUB)
 
-        def scatter_half(t, a):
-            move("S", f1[t][:].indirect(entries(list2, a)), r[t][:, slots(a)])
+        def scatter_half(t, half):
+            move("S", f1[t][:].indirect(entries(list2, half)), r[t][:, slots(half)])
 
-        def update(t, buffer):
-            c1[t] = tile(buffer, U, F32)
+        def update(t, after=None):
+            c1[t] = tile("c1_%d" % t, U, F32, after)
             nc.vector.scalar_tensor_tensor(out=c1[t][:], in0=f1[t][:], scalar=lam_t[:, t : t + 1], in1=h1[t][:], op0=MULT, op1=ADD)
 
-        def look_up_c1(t, a, engine):
-            move(engine, cg[a][:, t, :], c1[t][:].indirect(entries(list3, a)))
+        def look_up_c1(t, half, engine):
+            move(engine, c1_picked[half][:, t, :], c1[t][:].indirect(entries(list3, half)))
 
-        def weave(a):
-            nc.vector.tensor_tensor(out=woven[a][:].rearrange("p (c i t) -> p c t i", i=RUN, t=PACK),
-                                    in0=cg[a][:].rearrange("p t (c i) -> p c t i", i=RUN),
-                                    in1=kf_t[:].unsqueeze(1).unsqueeze(3).to_broadcast([P, HALF // RUN, PACK, RUN]), op=MULT)
+        def weave(half):
+            run = LINE // (2 * PACK)
+            nc.vector.tensor_tensor(out=w[half][:].rearrange("p (c i t) -> p c t i", i=run, t=PACK),
+                                    in0=c1_picked[half][:].rearrange("p t (c i) -> p c t i", i=run),
+                                    in1=kf_t[:].unsqueeze(1).unsqueeze(3).to_broadcast([P, HALF // run, PACK, run]), op=MULT)
 
-        def finish(a):
-            nc.vector.quantize_mx(out=wq_w[a][:].bitcast(FP8X4), scales=wq_s[a][:], in_=woven[a][:])
-            for e in range(2):
-                bank = bank_tile(2 * a + e, HALF)
-                nc.tensor.matmul_mx(out=bank[:], lhsT=wo_w[:, cols(e)].bitcast(FP8X4), lhsT_scale=wo_s[:, cols(e)],
-                                    rhs=wq_w[a][:].bitcast(FP8X4), rhs_scale=wq_s[a][:], start=True, stop=True)
-                y = tile("y_%d_%d" % (a, e), HALF, F32)
-                move("SV"[e], y[:], bank[:])
-                nc.sync.dma_start(out=out[cols(e), slots(a)], in_=y[:])
+        def outputs(half):
+            nc.vector.quantize_mx(out=wq_w[half][:].bitcast(FP8X4), scales=wq_s[half][:], in_=w[half][:])
+            for n in range(E // P):
+                bank = bank_tile(2 * half + n, HALF)
+                nc.tensor.matmul_mx(out=bank[:], lhsT=wo_w[:, cols(n)].bitcast(FP8X4), lhsT_scale=wo_s[:, cols(n)],
+                                    rhs=wq_w[half][:].bitcast(FP8X4), rhs_scale=wq_s[half][:], start=True, stop=True)
+                y = tile("y_%d_%d" % (half, n), HALF, F32)
+                move("SV"[n], y[:], bank[:])
+                nc.sync.dma_start(out=out[cols(n), slots(half)], in_=y[:])
 
-        deal(wb_wd, wb_w, 8)
-        deal(wb_sd, wb_s, 16)
-        f1[1] = f1[3] = sb.tile([P, U], F32, name="f1_1", tag="wb_w", align_bytes=64)
-        f1[2] = sb.tile([P, U], F32, name="f1_2", tag="wb_s", align_bytes=64)
+        deal(wb_w_dealt, wb_w, 2)
+        deal(wb_s_dealt, wb_s, 1)
+        f1[1] = tile("f1_1", U, F32, after="wb_w")
+        f1[2] = tile("f1_2", U, F32, after="wb_s")
         nc.vector.memset(f1[1][:], 0.0)
         nc.vector.memset(f1[2][:], 0.0)
-        hidden_notes(0, (0, 1), "SS", "h1_0")
+        hidden_notes(0, "S")
         nc.vector.tensor_copy(out=picked_w[:], in_=pages_w[:].indirect(list1[:]))
-        look_up_h1(0, 1.0, "hg_0")
+        f1[3] = tile("f1_3", U, F32, after="pages_w")
+        nc.gpsimd.memset(f1[3][:], 0.0)
+        look_up_h1(0, 1.0)
         nc.vector.tensor_copy(out=picked_s[:], in_=pages_s[:].indirect(list1[:]))
-        deal(wa_wd, wa_w, 4)
-        deal(wa_sd, wa_s, 16)
-        hidden_notes(1, (2, 3), "SS", "h1_1")
-        hidden_notes(2, (0, 1), "VV", "wa_s")
-        look_up_h1(1, 1.0, "hg_1")
-        hidden_notes(3, (2, 3), "SS", "h1_3")
-        for t in range(PACK):
+        deal(wa_w_dealt, wa_w, 4)
+        deal(wa_s_dealt, wa_s, 1)
+        hidden_notes(1, "S")
+        hidden_notes(2, "V", after="wa_s")
+        look_up_h1(1, 1.0)
+        hidden_notes(3, "S")
+        for t in (1, 0, 3, 2):
             hidden_pages(t)
-        look_up_h1(2, 1.0, "hg_2")
-        look_up_h1(3, -1.0, "hg_3")
-        difference(0)
-        difference(1)
+        look_up_h1(2, 1.0)
+        look_up_h1(3, -1.0)
+        for t in (1, 0, 2):
+            difference(t)
+        move("S", z_last[:], z_bank[3][:])
+
         scatter_half(0, 0)
-        difference(2)
         move("V", f1[1][:].indirect(list2[:]), r[1][:])
-        copy_z(3)
-        scatter_half(0, 1)
         scatter_half(2, 0)
-        update(1, "c1_1")
-        look_up_c1(1, 0, "S")
+        nc.vector.tensor_tensor(out=f1[3][:].indirect(list2[:]), in0=z_last[:], in1=h1_picked[3][:], op=ADD)
+        scatter_half(0, 1)
         scatter_half(2, 1)
-        nc.vector.tensor_tensor(out=f1[3][:].indirect(list2[:]), in0=r[3][:], in1=hg[3][:], op=ADD)
-        update(0, "hg_3")
-        look_up_c1(1, 1, "S")
-        update(3, "c1_3")
-        for a in range(2):
-            look_up_c1(0, a, "S")
-        update(2, "r_3")
+
+        update(1)
+        update(0, after="h1_picked_3")
+        for half in range(2):
+            look_up_c1(1, half, "S")
+        update(3)
+        for half in range(2):
+            look_up_c1(0, half, "S")
+        update(2, after="z_last")
         for t in (3, 2):
             look_up_c1(t, 0, "V")
             look_up_c1(t, 1, "S")
-        for a in range(2):
-            weave(a)
-            finish(a)
+        for half in range(2):
+            weave(half)
+            outputs(half)

from contextlib import ExitStack

import concourse.mybir as mybir

D, K, T, U, I, E = 512, 512, 2048, 1024, 512, 256
FLOPS = 2 * D * K * I + 2 * D * K * U + 2 * K * E * I

F32 = mybir.dt.float32
BF16 = mybir.dt.bfloat16
I32 = mybir.dt.int32
U32 = mybir.dt.uint32
U16 = mybir.dt.uint16
U8 = mybir.dt.uint8
FP8X4 = mybir.dt.float8_e4m3fn_x4
FP4X4 = mybir.dt.float4_e2m1fn_x4
MULT = mybir.AluOpType.mult
ADD = mybir.AluOpType.add
SUB = mybir.AluOpType.subtract
COPY = mybir.ActivationFunctionType.Copy

P = 128
PACK = 4
QUADRANTS = 4
BANK = 512
HALF = I // 2
LIST_COLS = I // 16
LINE = 16
FIRST_Z_BANK = 4


def tile_attend_pagesreplace_kernel(tc, pages_words, pages_scales, wa_words, wa_scales, notes_words, notes_scales,
                                     wb_words, wb_scales, lam, kf, wo_words, wo_scales, offs, offs2, offs3, out):
    nc = tc.nc
    with ExitStack() as ctx:
        sb = ctx.enter_context(tc.tile_pool(name="sb", bufs=1))
        ps = ctx.enter_context(tc.psum_pool(name="ps", bufs=1))

        def tile(name, width, dtype, after=None):
            return sb.tile([P, width], dtype, name=name, tag=after or name, align_bytes=64)

        def bank_tile(n, width):
            return ps.tile([P, width], F32, name="bank", tag="bank%d" % n)

        def cols(n):
            return slice(n * P, (n + 1) * P)

        def slots(half):
            return slice(half * HALF, (half + 1) * HALF)

        def entries(offsets, half):
            return offsets[:, half * LIST_COLS // 2 : (half + 1) * LIST_COLS // 2]

        def move(engine, dst, src):
            if engine == "S":
                nc.scalar.activation(out=dst, in_=src, func=COPY)
            else:
                nc.vector.tensor_copy(out=dst, in_=src)

        def load_words(dst, src):
            nc.sync.dma_start(out=dst[:].bitcast(I32), in_=src.bitcast(I32))

        def load_scales(dst, src, quadrants=range(QUADRANTS)):
            for q in quadrants:
                nc.sync.dma_start(out=dst[32 * q : 32 * q + 4, :].bitcast(I32), in_=src[0, 4 * q : 4 * q + 4, :].bitcast(I32))

        list1 = sb.tile([P, LIST_COLS], U16, name="list1")
        list2 = sb.tile([P, LIST_COLS], U16, name="list2")
        list3 = sb.tile([P, LIST_COLS], U16, name="list3")
        pages_w, pages_s = tile("pages_w", T, U16), tile("pages_s", T, U8)
        notes_w, notes_s = tile("notes_w", U, U32), tile("notes_s", U, U8)
        wa_w, wa_s = tile("wa_w", K, U32), tile("wa_s", K, U8)
        wb_w, wb_s = tile("wb_w", K, U16), tile("wb_s", K, U8)
        wo_w, wo_s = tile("wo_w", E, U32), tile("wo_s", E, U8)
        lam_t, kf_t = tile("lam_t", PACK, F32), tile("kf_t", PACK, F32)
        f1 = {0: tile("f1_0", U, F32)}

        for plane in (wb_s, pages_s, wa_s):
            nc.vector.memset(plane[:].bitcast(U32), 0)
        nc.vector.memset(f1[0][:], 0.0)

        load_words(wb_w, wb_words[0])
        load_scales(notes_s, notes_scales, range(QUADRANTS // 2))
        load_scales(wb_s, wb_scales)
        load_words(notes_w, notes_words[0].rearrange("p n t -> p (n t)"))
        load_scales(notes_s, notes_scales, range(QUADRANTS // 2, QUADRANTS))
        nc.sync.dma_start(out=list1[:], in_=offs)
        load_words(pages_w, pages_words[0])
        nc.sync.dma_start(out=list2[:], in_=offs2)
        load_scales(pages_s, pages_scales)
        load_words(wa_w, wa_words[0].rearrange("p n t -> p (n t)"))
        load_scales(wa_s, wa_scales)
        nc.sync.dma_start(out=lam_t[:], in_=lam.rearrange("(p t) o -> p (t o)", t=PACK))
        nc.sync.dma_start(out=list3[:], in_=offs3)
        nc.sync.dma_start(out=kf_t[:], in_=kf.rearrange("(p t) o -> p (t o)", t=PACK))
        load_words(wo_w, wo_words[0].rearrange("p n t -> p (n t)"))
        load_scales(wo_s, wo_scales)

        wb_w_dealt, wb_s_dealt = tile("wb_w_dealt", K, U16), tile("wb_s_dealt", K, U8)
        wa_w_dealt, wa_s_dealt = tile("wa_w_dealt", K, U32), tile("wa_s_dealt", K, U8)
        picked_w, picked_s = tile("picked_w", I, U16), tile("picked_s", I, U8)
        r = [tile("r_%d" % t, I, F32) for t in range(PACK - 1)]
        z_last = tile("z_last", I, F32)
        c1_picked = [sb.tile([P, PACK, HALF], F32, name="c1_picked_%d" % half, align_bytes=64) for half in range(2)]
        w = [tile("w_%d" % half, HALF * PACK, BF16) for half in range(2)]
        wq_w = [tile("wq_w_%d" % half, HALF, U32) for half in range(2)]
        wq_s = [tile("wq_s_%d" % half, HALF, U8) for half in range(2)]
        h1, c1, z_bank, h1_picked = {}, {}, {}, {}

        def deal(dst, src, item_bytes):
            run = LINE // item_bytes
            nc.vector.tensor_copy(out=dst[:].rearrange("p (t c i) -> p c t i", t=PACK, i=run),
                                  in_=src[:].rearrange("p (c i t) -> p c t i", t=PACK, i=run))

        def hidden_notes(t, engine, after=None):
            h1[t] = tile("h1_%d" % t, U, F32, after)
            for b in range(U // BANK):
                bank = bank_tile(2 * (t % 2) + b, BANK)
                notes = slice(b * BANK, (b + 1) * BANK)
                nc.tensor.matmul_mx(out=bank[:], lhsT=wb_w_dealt[:, cols(t)].bitcast(FP4X4), lhsT_scale=wb_s_dealt[:, cols(t)],
                                    rhs=notes_w[:, notes].bitcast(FP8X4), rhs_scale=notes_s[:, notes], start=True, stop=True)
                move(engine, h1[t][:, notes], bank[:])

        def hidden_pages(t):
            z_bank[t] = bank_tile(FIRST_Z_BANK + t, I)
            nc.tensor.matmul_mx(out=z_bank[t][:], lhsT=wa_w_dealt[:, cols(t)].bitcast(FP8X4), lhsT_scale=wa_s_dealt[:, cols(t)],
                                rhs=picked_w[:].bitcast(FP4X4), rhs_scale=picked_s[:], start=True, stop=True)

        def look_up_h1(t, sign):
            h1_picked[t] = tile("h1_picked_%d" % t, I, F32)
            nc.scalar.activation(out=h1_picked[t][:], in_=h1[t][:].indirect(list2[:]), func=COPY, scale=sign)

        def difference(t):
            nc.vector.tensor_tensor(out=r[t][:], in0=z_bank[t][:], in1=h1_picked[t][:], op=SUB)

        def scatter_half(t, half):
            move("S", f1[t][:].indirect(entries(list2, half)), r[t][:, slots(half)])

        def update(t, after=None):
            c1[t] = tile("c1_%d" % t, U, F32, after)
            nc.vector.scalar_tensor_tensor(out=c1[t][:], in0=f1[t][:], scalar=lam_t[:, t : t + 1], in1=h1[t][:], op0=MULT, op1=ADD)

        def look_up_c1(t, half, engine):
            move(engine, c1_picked[half][:, t, :], c1[t][:].indirect(entries(list3, half)))

        def weave(half):
            run = LINE // (2 * PACK)
            nc.vector.tensor_tensor(out=w[half][:].rearrange("p (c i t) -> p c t i", i=run, t=PACK),
                                    in0=c1_picked[half][:].rearrange("p t (c i) -> p c t i", i=run),
                                    in1=kf_t[:].unsqueeze(1).unsqueeze(3).to_broadcast([P, HALF // run, PACK, run]), op=MULT)

        def outputs(half):
            nc.vector.quantize_mx(out=wq_w[half][:].bitcast(FP8X4), scales=wq_s[half][:], in_=w[half][:])
            for n in range(E // P):
                bank = bank_tile(2 * half + n, HALF)
                nc.tensor.matmul_mx(out=bank[:], lhsT=wo_w[:, cols(n)].bitcast(FP8X4), lhsT_scale=wo_s[:, cols(n)],
                                    rhs=wq_w[half][:].bitcast(FP8X4), rhs_scale=wq_s[half][:], start=True, stop=True)
                y = tile("y_%d_%d" % (half, n), HALF, F32)
                move("SV"[n], y[:], bank[:])
                nc.sync.dma_start(out=out[cols(n), slots(half)], in_=y[:])

        deal(wb_w_dealt, wb_w, 2)
        deal(wb_s_dealt, wb_s, 1)
        f1[1] = tile("f1_1", U, F32, after="wb_w")
        f1[2] = tile("f1_2", U, F32, after="wb_s")
        nc.vector.memset(f1[1][:], 0.0)
        nc.vector.memset(f1[2][:], 0.0)
        hidden_notes(0, "S")
        nc.vector.tensor_copy(out=picked_w[:], in_=pages_w[:].indirect(list1[:]))
        f1[3] = tile("f1_3", U, F32, after="pages_w")
        nc.gpsimd.memset(f1[3][:], 0.0)
        look_up_h1(0, 1.0)
        nc.vector.tensor_copy(out=picked_s[:], in_=pages_s[:].indirect(list1[:]))
        deal(wa_w_dealt, wa_w, 4)
        deal(wa_s_dealt, wa_s, 1)
        hidden_notes(1, "S")
        hidden_notes(2, "V", after="wa_s")
        look_up_h1(1, 1.0)
        hidden_notes(3, "S")
        for t in (1, 0, 3, 2):
            hidden_pages(t)
        look_up_h1(2, 1.0)
        look_up_h1(3, -1.0)
        for t in (1, 0, 2):
            difference(t)
        move("S", z_last[:], z_bank[3][:])

        scatter_half(0, 0)
        move("V", f1[1][:].indirect(list2[:]), r[1][:])
        scatter_half(2, 0)
        nc.vector.tensor_tensor(out=f1[3][:].indirect(list2[:]), in0=z_last[:], in1=h1_picked[3][:], op=ADD)
        scatter_half(0, 1)
        scatter_half(2, 1)

        update(1)
        update(0, after="h1_picked_3")
        for half in range(2):
            look_up_c1(1, half, "S")
        update(3)
        for half in range(2):
            look_up_c1(0, half, "S")
        update(2, after="z_last")
        for t in (3, 2):
            look_up_c1(t, 0, "V")
            look_up_c1(t, 1, "S")
        for half in range(2):
            weave(half)
            outputs(half)
